import numpy as np
import ml_dtypes


def mxq(x, axis, fmt="e4m3"):
    dtype, down = {"e4m3": (ml_dtypes.float8_e4m3fn, 7), "e5m2": (ml_dtypes.float8_e5m2, 14)}[fmt]
    v = np.moveaxis(np.asarray(x, np.float32).astype(ml_dtypes.bfloat16).astype(np.float64), axis, -1)
    blocks = v.reshape(v.shape[:-1] + (-1, 32))
    amax = np.abs(blocks).max(-1, keepdims=True)
    byte = np.maximum(np.where(amax > 0, np.frexp(amax)[1] - 1 + 127, 0) - down, 1)
    scale = np.exp2(byte - 127.0)
    codes = (blocks / scale).astype(np.float32).astype(dtype).astype(np.float64)
    return np.moveaxis((codes * scale).reshape(v.shape), -1, axis)


WIDE = False


def mx_kscale(k):
    if not WIDE:
        return np.ones(k)
    levels = np.array([30, -30])
    if k % 512:
        return np.exp2(np.random.permutation(np.resize(levels, k // 32))).repeat(32)
    a = np.empty((k // 512, 16))
    for p in range(k // 512):
        a[p, :8] = np.random.permutation(np.resize(levels, 8))
        for g in range(8):
            far = levels[np.abs(levels - a[p, g]) >= 10]
            a[p, g + 8] = far[np.random.randint(len(far))]
    return np.exp2(a.ravel()).repeat(32)


def f64(x):
    return np.asarray(x).astype(np.float64)


def striped(idx):
    return np.tile(np.asarray(idx).reshape(-1, 16).T, (8, 1)).astype(np.uint16)


def unstriped(offs):
    return offs[:16].T.reshape(-1).astype(np.int64)


K, N, T, S, J, B = 512, 512, 1024, 1024, 2048, 512


def setup_inputs():
    n = np.random.standard_normal
    idx = np.random.randint(0, T, J)
    idx2 = np.random.randint(0, S, J)
    fb = mx_kscale(B)
    return {
        "xf": (n((K, T))).astype(np.float32),
        "xo": (n((N, S))).astype(np.float32),
        "ra": (np.random.uniform(0.3, 1.0, (1, B)) * fb).astype(np.float32),
        "rb": (np.random.uniform(0.3, 1.0, (1, B)) / fb).astype(np.float32),
        "offs": striped(idx),
        "offs2": striped(idx2),
    }


def reference(xf, xo, ra, rb, offs, offs2):
    idx = unstriped(offs)
    idx2 = unstriped(offs2)
    sa = f64(xf)[:, idx].reshape(K, B, J // B).sum(axis=2) * f64(ra)
    sb = f64(xo)[:, idx2].reshape(N, B, J // B).sum(axis=2) * f64(rb)
    at = sa.T
    bt = sb.T
    atq = mxq(at, 0, "e4m3")
    btq = mxq(bt, 0, "e5m2")
    w = atq.T @ btq
    y = 0.03 * w
    return y

@@ -1,0 +1,146 @@
+from contextlib import ExitStack
+
+import concourse.mybir as mybir
+from concourse.masks import make_identity
+
+K, N, T, J, B = 512, 512, 1024, 2048, 512
+FLOPS = 2 * K * N * B
+
+F32 = mybir.dt.float32
+BF16 = mybir.dt.bfloat16
+U32 = mybir.dt.uint32
+U16 = mybir.dt.uint16
+U8 = mybir.dt.uint8
+E4M3 = mybir.dt.float8_e4m3fn_x4
+E5M2 = mybir.dt.float8_e5m2_x4
+COPY = mybir.ActivationFunctionType.Copy
+MULT = mybir.AluOpType.mult
+
+P = 128
+PACK = 4
+GROUP = 4
+ROWS = 8
+BLOCKS = 16
+OUT_SCALE = 0.03
+PIECES = ((0, 6), (6, 12), (12, 16))
+COLS_PER_BLOCK = 8
+
+
+def tile_moe_expert_group_sums_wgrad_kernel(tc, xf, xo, ra, rb, offs, offs2, out):
+    nc = tc.nc
+    with ExitStack() as ctx:
+        keep = ctx.enter_context(tc.tile_pool(name="keep", bufs=1))
+        sums_psum = ctx.enter_context(tc.psum_pool(name="sums_psum", bufs=3))
+        prod_psum = ctx.enter_context(tc.psum_pool(name="prod_psum", bufs=1))
+
+        list_f = keep.tile([P, J // 16], U16, name="list_f")
+        list_o = keep.tile([P, J // 16], U16, name="list_o")
+        win_o = [keep.tile([P, T], F32, name="win_o%d" % i) for i in range(4)]
+        win_f = [keep.tile([P, T], F32, name="win_f%d" % i) for i in range(4)]
+        weight_rows = keep.tile([P, P], F32, name="weight_rows")
+        ident = keep.tile([P, P], F32, name="ident")
+        weights = keep.tile([P, 2 * PACK], F32, name="weights")
+
+        nc.gpsimd.memset(weight_rows[:], 0.0)
+        make_identity(nc, ident[:])
+
+        nc.sync.dma_start(out=win_o[0][:], in_=xo[0:P, :])
+        nc.sync.dma_start(list_o[:], offs2)
+        nc.sync.dma_start(out=win_o[1][:], in_=xo[P : 2 * P, :])
+        for row0, vec in ((0, ra), (PACK, rb)):
+            nc.sync.dma_start(
+                out=weight_rows[row0 : row0 + PACK, :].rearrange("t (q r) -> t q r", r=ROWS),
+                in_=vec.rearrange("o (q t r) -> (o t) q r", t=PACK, r=ROWS),
+            )
+        for i in range(2, 4):
+            nc.sync.dma_start(out=win_o[i][:], in_=xo[i * P : (i + 1) * P, :])
+        nc.sync.dma_start(list_f[:], offs)
+        for i in range(4):
+            nc.sync.dma_start(out=win_f[i][:], in_=xf[i * P : (i + 1) * P, :])
+
+        weights_psum = prod_psum.tile([P, P], F32, name="weights_psum")
+        nc.tensor.transpose(weights_psum[:], weight_rows[:], ident[:])
+        nc.scalar.copy(out=weights[:], in_=weights_psum[:, 0 : 2 * PACK])
+
+        def group_sums(window, offsets, name):
+            picked = keep.tile([P, J], F32, name=name)
+            planes = picked[:].bitcast(U32).rearrange(
+                "p (t u q r) -> p q t r u", t=PACK, u=GROUP, r=ROWS
+            )
+            for q0, q1 in PIECES:
+                nc.vector.tensor_copy(
+                    planes[:, q0:q1],
+                    window[:].bitcast(U32).indirect(offsets[:, q0 * COLS_PER_BLOCK : q1 * COLS_PER_BLOCK]),
+                )
+            sums = sums_psum.tile([P, PACK, P], F32, name="sums")
+            for t in range(PACK):
+                for u in range(GROUP):
+                    c0 = (t * GROUP + u) * P
+                    nc.tensor.matmul(
+                        sums[:, t, :], picked[:, c0 : c0 + P], ident[:],
+                        start=(u == 0), stop=(u == GROUP - 1), is_transpose=True,
+                    )
+            return sums
+
+        def weigh_on_scalar(sums, rounded, col0):
+            for t in range(PACK):
+                nc.scalar.activation(
+                    out=rounded[:, :, t], in_=sums[:, t, :], func=COPY,
+                    scale=weights[:, col0 + t : col0 + t + 1],
+                )
+
+        b_rounded = keep.tile([P, N, PACK], BF16, name="b_rounded", align_bytes=64)
+        a01_rounded = keep.tile([P, 2 * P, PACK], BF16, name="a01_rounded", align_bytes=64)
+        a2_rounded = keep.tile([P, P, PACK], BF16, name="a2_rounded", align_bytes=64)
+        a3_rounded = keep.tile([P, P, PACK], BF16, name="a3_rounded", align_bytes=64)
+
+        for i in range(4):
+            sums = group_sums(win_o[i], list_o, "picked_o%d" % i)
+            weigh_on_scalar(sums, b_rounded[:, i * P : (i + 1) * P, :], PACK)
+        for i in range(2):
+            sums = group_sums(win_f[i], list_f, "picked_f%d" % i)
+            weigh_on_scalar(sums, a01_rounded[:, i * P : (i + 1) * P, :], 0)
+        sums = group_sums(win_f[2], list_f, "picked_f2")
+        weigh_on_scalar(sums, a2_rounded[:], 0)
+        last_sums = group_sums(win_f[3], list_f, "picked_f3")
+
+        def quantize(rounded, width, fmt, name):
+            codes = keep.tile([P, width], U32, name=name + "_codes", align_bytes=64)
+            scales = keep.tile([P, width], U8, name=name + "_scales", align_bytes=64)
+            nc.vector.quantize_mx(
+                out=codes[:].bitcast(fmt), scales=scales[:],
+                in_=rounded[:].rearrange("p c t -> p (c t)"),
+            )
+            return codes, scales
+
+        b_codes, b_scales = quantize(b_rounded, N, E5M2, "b")
+        a01 = quantize(a01_rounded, 2 * P, E4M3, "a01")
+        a2 = quantize(a2_rounded, P, E4M3, "a2")
+        nc.vector.tensor_tensor(
+            out=a3_rounded[:], in0=last_sums[:].rearrange("p t k -> p k t"),
+            in1=weights[:, 0:PACK].unsqueeze(1).to_broadcast([P, P, PACK]), op=MULT,
+        )
+        a3 = quantize(a3_rounded, P, E4M3, "a3")
+
+        stationary = ((a01, 0), (a01, P), (a2, 0), (a3, 0))
+        for i, ((codes, scales), c0) in enumerate(stationary):
+            product = prod_psum.tile([P, N], F32, name="product%d" % i)
+            nc.tensor.matmul_mx(
+                out=product[:],
+                lhsT=codes[:, c0 : c0 + P].bitcast(E4M3), lhsT_scale=scales[:, c0 : c0 + P],
+                rhs=b_codes[:].bitcast(E5M2), rhs_scale=b_scales[:],
+                start=True, stop=True,
+            )
+            rows = slice(i * P, (i + 1) * P)
+            if i < 3:
+                result = keep.tile([P, N], F32, name="result%d" % i)
+                nc.scalar.activation(out=result[:], in_=product[:], func=COPY, scale=OUT_SCALE)
+                nc.sync.dma_start(out=out[rows, :], in_=result[:])
+            else:
+                for h in range(2):
+                    cols = slice(h * N // 2, (h + 1) * N // 2)
+                    result = keep.tile([P, N // 2], F32, name="last_result%d" % h)
+                    nc.vector.tensor_scalar(
+                        out=result[:], in0=product[:, cols], scalar1=OUT_SCALE, scalar2=None, op0=MULT
+                    )
+                    nc.sync.dma_start(out=out[rows, cols], in_=result[:])

@@ -22,7 +22,7 @@ GROUP = 4
 ROWS = 8
 BLOCKS = 16
 OUT_SCALE = 0.03
-PIECES = ((0, 6), (6, 12), (12, 16))
+EARLY_BLOCKS = 12
 COLS_PER_BLOCK = 8
 
 
@@ -35,43 +35,63 @@ def tile_moe_expert_group_sums_wgrad_kernel(tc, xf, xo, ra, rb, offs, offs2, out
 
         list_f = keep.tile([P, J // 16], U16, name="list_f")
         list_o = keep.tile([P, J // 16], U16, name="list_o")
-        win_o = [keep.tile([P, T], F32, name="win_o%d" % i) for i in range(4)]
-        win_f = [keep.tile([P, T], F32, name="win_f%d" % i) for i in range(4)]
+        table_o = keep.tile([P, 5 * T], F32, name="table_o")
+        table_f = keep.tile([P, 5 * T], F32, name="table_f")
+        last_picked = keep.tile([P, J], F32, name="last_picked")
+        late_sums = keep.tile([P, PACK, P], F32, name="late_sums")
         weight_rows = keep.tile([P, P], F32, name="weight_rows")
         ident = keep.tile([P, P], F32, name="ident")
         weights = keep.tile([P, 2 * PACK], F32, name="weights")
 
+        nc.vector.memset(table_o[:, 4 * T :], 0.0)
+        nc.vector.memset(table_f[:, 4 * T :], 0.0)
+        nc.vector.memset(
+            last_picked[:].rearrange("p (c m) -> p c m", m=P)[:, :, EARLY_BLOCKS * ROWS :], 0.0
+        )
+        nc.vector.memset(late_sums[:], 0.0)
         nc.gpsimd.memset(weight_rows[:], 0.0)
         make_identity(nc, ident[:])
 
-        nc.sync.dma_start(out=win_o[0][:], in_=xo[0:P, :])
+        def load(table, source, i):
+            nc.sync.dma_start(out=table[:, i * T : (i + 1) * T], in_=source[i * P : (i + 1) * P, :])
+
+        load(table_o, xo, 3)
         nc.sync.dma_start(list_o[:], offs2)
-        nc.sync.dma_start(out=win_o[1][:], in_=xo[P : 2 * P, :])
+        load(table_o, xo, 2)
         for row0, vec in ((0, ra), (PACK, rb)):
             nc.sync.dma_start(
                 out=weight_rows[row0 : row0 + PACK, :].rearrange("t (q r) -> t q r", r=ROWS),
                 in_=vec.rearrange("o (q t r) -> (o t) q r", t=PACK, r=ROWS),
             )
-        for i in range(2, 4):
-            nc.sync.dma_start(out=win_o[i][:], in_=xo[i * P : (i + 1) * P, :])
+        load(table_o, xo, 1)
+        load(table_o, xo, 0)
         nc.sync.dma_start(list_f[:], offs)
         for i in range(4):
-            nc.sync.dma_start(out=win_f[i][:], in_=xf[i * P : (i + 1) * P, :])
+            load(table_f, xf, i)
 
         weights_psum = prod_psum.tile([P, P], F32, name="weights_psum")
         nc.tensor.transpose(weights_psum[:], weight_rows[:], ident[:])
         nc.scalar.copy(out=weights[:], in_=weights_psum[:, 0 : 2 * PACK])
 
-        def group_sums(window, offsets, name):
-            picked = keep.tile([P, J], F32, name=name)
-            planes = picked[:].bitcast(U32).rearrange(
+        def planes_of(picked):
+            return picked[:].bitcast(U32).rearrange(
                 "p (t u q r) -> p q t r u", t=PACK, u=GROUP, r=ROWS
             )
-            for q0, q1 in PIECES:
-                nc.vector.tensor_copy(
-                    planes[:, q0:q1],
-                    window[:].bitcast(U32).indirect(offsets[:, q0 * COLS_PER_BLOCK : q1 * COLS_PER_BLOCK]),
-                )
+
+        def gather(dst, table, i, width, offsets, q0, q1):
+            window = table[:, i * T : i * T + width].bitcast(U32)
+            nc.vector.tensor_copy(
+                dst, window.indirect(offsets[:, q0 * COLS_PER_BLOCK : q1 * COLS_PER_BLOCK])
+            )
+
+        def group_sums(table, i, offsets, name):
+            picked = keep.tile([P, J], F32, name=name)
+            planes = planes_of(picked)
+            if i < 2:
+                gather(planes, table, i, 4 * T, offsets, 0, BLOCKS)
+            else:
+                gather(planes[:, :EARLY_BLOCKS], table, i, 2 * T, offsets, 0, EARLY_BLOCKS)
+                gather(planes[:, EARLY_BLOCKS:], table, i, 2 * T, offsets, EARLY_BLOCKS, BLOCKS)
             sums = sums_psum.tile([P, PACK, P], F32, name="sums")
             for t in range(PACK):
                 for u in range(GROUP):
@@ -80,6 +100,32 @@ def tile_moe_expert_group_sums_wgrad_kernel(tc, xf, xo, ra, rb, offs, offs2, out
                         sums[:, t, :], picked[:, c0 : c0 + P], ident[:],
                         start=(u == 0), stop=(u == GROUP - 1), is_transpose=True,
                     )
+            return sums
+
+        def last_group_sums(table, i, offsets):
+            late = BLOCKS - EARLY_BLOCKS
+            gather(planes_of(last_picked)[:, :EARLY_BLOCKS], table, i, 2 * T, offsets, 0, EARLY_BLOCKS)
+            late_picked = keep.tile([P, late * P], F32, name="late_picked")
+            gather(
+                late_picked[:].bitcast(U32).rearrange("p (t q c) -> p q t c", t=PACK, q=late),
+                table, i, 2 * T, offsets, EARLY_BLOCKS, BLOCKS,
+            )
+            nc.vector.tensor_reduce(
+                out=late_sums[:, :, EARLY_BLOCKS * ROWS :],
+                in_=late_picked[:].rearrange("p (t m u) -> p t m u", t=PACK, u=GROUP),
+                axis=mybir.AxisListType.X, op=mybir.AluOpType.add,
+            )
+            sums = sums_psum.tile([P, PACK, P], F32, name="sums")
+            for c in range(PACK * GROUP):
+                nc.tensor.matmul(
+                    sums[:, c // GROUP, :], last_picked[:, c * P : (c + 1) * P], ident[:],
+                    start=(c == 0), stop=False, is_transpose=True,
+                )
+            for t in range(PACK):
+                nc.tensor.matmul(
+                    sums[:, t, :], late_sums[:, t, :], ident[:],
+                    start=False, stop=(t == PACK - 1), is_transpose=True,
+                )
             return sums
 
         def weigh_on_scalar(sums, rounded, col0):
@@ -94,15 +140,15 @@ def tile_moe_expert_group_sums_wgrad_kernel(tc, xf, xo, ra, rb, offs, offs2, out
         a2_rounded = keep.tile([P, P, PACK], BF16, name="a2_rounded", align_bytes=64)
         a3_rounded = keep.tile([P, P, PACK], BF16, name="a3_rounded", align_bytes=64)
 
-        for i in range(4):
-            sums = group_sums(win_o[i], list_o, "picked_o%d" % i)
+        for i in (3, 2, 1, 0):
+            sums = group_sums(table_o, i, list_o, "picked_o%d" % i)
             weigh_on_scalar(sums, b_rounded[:, i * P : (i + 1) * P, :], PACK)
         for i in range(2):
-            sums = group_sums(win_f[i], list_f, "picked_f%d" % i)
+            sums = group_sums(table_f, i, list_f, "picked_f%d" % i)
             weigh_on_scalar(sums, a01_rounded[:, i * P : (i + 1) * P, :], 0)
-        sums = group_sums(win_f[2], list_f, "picked_f2")
+        sums = group_sums(table_f, 2, list_f, "picked_f2")
         weigh_on_scalar(sums, a2_rounded[:], 0)
-        last_sums = group_sums(win_f[3], list_f, "picked_f3")
+        last_sums = last_group_sums(table_f, 3, list_f)
 
         def quantize(rounded, width, fmt, name):
             codes = keep.tile([P, width], U32, name=name + "_codes", align_bytes=64)

from contextlib import ExitStack

import concourse.mybir as mybir
from concourse.masks import make_identity

K, N, T, J, B = 512, 512, 1024, 2048, 512
FLOPS = 2 * K * N * B

F32 = mybir.dt.float32
BF16 = mybir.dt.bfloat16
U32 = mybir.dt.uint32
U16 = mybir.dt.uint16
U8 = mybir.dt.uint8
E4M3 = mybir.dt.float8_e4m3fn_x4
E5M2 = mybir.dt.float8_e5m2_x4
COPY = mybir.ActivationFunctionType.Copy
MULT = mybir.AluOpType.mult

P = 128
PACK = 4
GROUP = 4
ROWS = 8
BLOCKS = 16
OUT_SCALE = 0.03
EARLY_BLOCKS = 12
COLS_PER_BLOCK = 8


def tile_moe_expert_group_sums_wgrad_kernel(tc, xf, xo, ra, rb, offs, offs2, out):
    nc = tc.nc
    with ExitStack() as ctx:
        keep = ctx.enter_context(tc.tile_pool(name="keep", bufs=1))
        sums_psum = ctx.enter_context(tc.psum_pool(name="sums_psum", bufs=3))
        prod_psum = ctx.enter_context(tc.psum_pool(name="prod_psum", bufs=1))

        list_f = keep.tile([P, J // 16], U16, name="list_f")
        list_o = keep.tile([P, J // 16], U16, name="list_o")
        table_o = keep.tile([P, 5 * T], F32, name="table_o")
        table_f = keep.tile([P, 5 * T], F32, name="table_f")
        last_picked = keep.tile([P, J], F32, name="last_picked")
        late_sums = keep.tile([P, PACK, P], F32, name="late_sums")
        weight_rows = keep.tile([P, P], F32, name="weight_rows")
        ident = keep.tile([P, P], F32, name="ident")
        weights = keep.tile([P, 2 * PACK], F32, name="weights")

        nc.vector.memset(table_o[:, 4 * T :], 0.0)
        nc.vector.memset(table_f[:, 4 * T :], 0.0)
        nc.vector.memset(
            last_picked[:].rearrange("p (c m) -> p c m", m=P)[:, :, EARLY_BLOCKS * ROWS :], 0.0
        )
        nc.vector.memset(late_sums[:], 0.0)
        nc.gpsimd.memset(weight_rows[:], 0.0)
        make_identity(nc, ident[:])

        def load(table, source, i):
            nc.sync.dma_start(out=table[:, i * T : (i + 1) * T], in_=source[i * P : (i + 1) * P, :])

        load(table_o, xo, 3)
        nc.sync.dma_start(list_o[:], offs2)
        load(table_o, xo, 2)
        for row0, vec in ((0, ra), (PACK, rb)):
            nc.sync.dma_start(
                out=weight_rows[row0 : row0 + PACK, :].rearrange("t (q r) -> t q r", r=ROWS),
                in_=vec.rearrange("o (q t r) -> (o t) q r", t=PACK, r=ROWS),
            )
        load(table_o, xo, 1)
        load(table_o, xo, 0)
        nc.sync.dma_start(list_f[:], offs)
        for i in range(4):
            load(table_f, xf, i)

        weights_psum = prod_psum.tile([P, P], F32, name="weights_psum")
        nc.tensor.transpose(weights_psum[:], weight_rows[:], ident[:])
        nc.scalar.copy(out=weights[:], in_=weights_psum[:, 0 : 2 * PACK])

        def planes_of(picked):
            return picked[:].bitcast(U32).rearrange(
                "p (t u q r) -> p q t r u", t=PACK, u=GROUP, r=ROWS
            )

        def gather(dst, table, i, width, offsets, q0, q1):
            window = table[:, i * T : i * T + width].bitcast(U32)
            nc.vector.tensor_copy(
                dst, window.indirect(offsets[:, q0 * COLS_PER_BLOCK : q1 * COLS_PER_BLOCK])
            )

        def group_sums(table, i, offsets, name):
            picked = keep.tile([P, J], F32, name=name)
            planes = planes_of(picked)
            if i < 2:
                gather(planes, table, i, 4 * T, offsets, 0, BLOCKS)
            else:
                gather(planes[:, :EARLY_BLOCKS], table, i, 2 * T, offsets, 0, EARLY_BLOCKS)
                gather(planes[:, EARLY_BLOCKS:], table, i, 2 * T, offsets, EARLY_BLOCKS, BLOCKS)
            sums = sums_psum.tile([P, PACK, P], F32, name="sums")
            for t in range(PACK):
                for u in range(GROUP):
                    c0 = (t * GROUP + u) * P
                    nc.tensor.matmul(
                        sums[:, t, :], picked[:, c0 : c0 + P], ident[:],
                        start=(u == 0), stop=(u == GROUP - 1), is_transpose=True,
                    )
            return sums

        def last_group_sums(table, i, offsets):
            late = BLOCKS - EARLY_BLOCKS
            gather(planes_of(last_picked)[:, :EARLY_BLOCKS], table, i, 2 * T, offsets, 0, EARLY_BLOCKS)
            late_picked = keep.tile([P, late * P], F32, name="late_picked")
            gather(
                late_picked[:].bitcast(U32).rearrange("p (t q c) -> p q t c", t=PACK, q=late),
                table, i, 2 * T, offsets, EARLY_BLOCKS, BLOCKS,
            )
            nc.vector.tensor_reduce(
                out=late_sums[:, :, EARLY_BLOCKS * ROWS :],
                in_=late_picked[:].rearrange("p (t m u) -> p t m u", t=PACK, u=GROUP),
                axis=mybir.AxisListType.X, op=mybir.AluOpType.add,
            )
            sums = sums_psum.tile([P, PACK, P], F32, name="sums")
            for c in range(PACK * GROUP):
                nc.tensor.matmul(
                    sums[:, c // GROUP, :], last_picked[:, c * P : (c + 1) * P], ident[:],
                    start=(c == 0), stop=False, is_transpose=True,
                )
            for t in range(PACK):
                nc.tensor.matmul(
                    sums[:, t, :], late_sums[:, t, :], ident[:],
                    start=False, stop=(t == PACK - 1), is_transpose=True,
                )
            return sums

        def weigh_on_scalar(sums, rounded, col0):
            for t in range(PACK):
                nc.scalar.activation(
                    out=rounded[:, :, t], in_=sums[:, t, :], func=COPY,
                    scale=weights[:, col0 + t : col0 + t + 1],
                )

        b_rounded = keep.tile([P, N, PACK], BF16, name="b_rounded", align_bytes=64)
        a01_rounded = keep.tile([P, 2 * P, PACK], BF16, name="a01_rounded", align_bytes=64)
        a2_rounded = keep.tile([P, P, PACK], BF16, name="a2_rounded", align_bytes=64)
        a3_rounded = keep.tile([P, P, PACK], BF16, name="a3_rounded", align_bytes=64)

        for i in (3, 2, 1, 0):
            sums = group_sums(table_o, i, list_o, "picked_o%d" % i)
            weigh_on_scalar(sums, b_rounded[:, i * P : (i + 1) * P, :], PACK)
        for i in range(2):
            sums = group_sums(table_f, i, list_f, "picked_f%d" % i)
            weigh_on_scalar(sums, a01_rounded[:, i * P : (i + 1) * P, :], 0)
        sums = group_sums(table_f, 2, list_f, "picked_f2")
        weigh_on_scalar(sums, a2_rounded[:], 0)
        last_sums = last_group_sums(table_f, 3, list_f)

        def quantize(rounded, width, fmt, name):
            codes = keep.tile([P, width], U32, name=name + "_codes", align_bytes=64)
            scales = keep.tile([P, width], U8, name=name + "_scales", align_bytes=64)
            nc.vector.quantize_mx(
                out=codes[:].bitcast(fmt), scales=scales[:],
                in_=rounded[:].rearrange("p c t -> p (c t)"),
            )
            return codes, scales

        b_codes, b_scales = quantize(b_rounded, N, E5M2, "b")
        a01 = quantize(a01_rounded, 2 * P, E4M3, "a01")
        a2 = quantize(a2_rounded, P, E4M3, "a2")
        nc.vector.tensor_tensor(
            out=a3_rounded[:], in0=last_sums[:].rearrange("p t k -> p k t"),
            in1=weights[:, 0:PACK].unsqueeze(1).to_broadcast([P, P, PACK]), op=MULT,
        )
        a3 = quantize(a3_rounded, P, E4M3, "a3")

        stationary = ((a01, 0), (a01, P), (a2, 0), (a3, 0))
        for i, ((codes, scales), c0) in enumerate(stationary):
            product = prod_psum.tile([P, N], F32, name="product%d" % i)
            nc.tensor.matmul_mx(
                out=product[:],
                lhsT=codes[:, c0 : c0 + P].bitcast(E4M3), lhsT_scale=scales[:, c0 : c0 + P],
                rhs=b_codes[:].bitcast(E5M2), rhs_scale=b_scales[:],
                start=True, stop=True,
            )
            rows = slice(i * P, (i + 1) * P)
            if i < 3:
                result = keep.tile([P, N], F32, name="result%d" % i)
                nc.scalar.activation(out=result[:], in_=product[:], func=COPY, scale=OUT_SCALE)
                nc.sync.dma_start(out=out[rows, :], in_=result[:])
            else:
                for h in range(2):
                    cols = slice(h * N // 2, (h + 1) * N // 2)
                    result = keep.tile([P, N // 2], F32, name="last_result%d" % h)
                    nc.vector.tensor_scalar(
                        out=result[:], in0=product[:, cols], scalar1=OUT_SCALE, scalar2=None, op0=MULT
                    )
                    nc.sync.dma_start(out=out[rows, cols], in_=result[:])
